import numpy as np
import ml_dtypes


def mxq(x, axis, fmt="e4m3"):
    dtype, down = {"e4m3": (ml_dtypes.float8_e4m3fn, 7), "e5m2": (ml_dtypes.float8_e5m2, 14)}[fmt]
    v = np.moveaxis(np.asarray(x, np.float32).astype(ml_dtypes.bfloat16).astype(np.float64), axis, -1)
    blocks = v.reshape(v.shape[:-1] + (-1, 32))
    amax = np.abs(blocks).max(-1, keepdims=True)
    byte = np.maximum(np.where(amax > 0, np.frexp(amax)[1] - 1 + 127, 0) - down, 1)
    scale = np.exp2(byte - 127.0)
    codes = (blocks / scale).astype(np.float32).astype(dtype).astype(np.float64)
    return np.moveaxis((codes * scale).reshape(v.shape), -1, axis)


WIDE = False


def mx_kscale(k):
    if not WIDE:
        return np.ones(k)
    levels = np.array([10, -10, 5, -5, 0])
    if k % 512:
        return np.exp2(np.random.permutation(np.resize(levels, k // 32))).repeat(32)
    a = np.empty((k // 512, 16))
    for p in range(k // 512):
        a[p, :8] = np.random.permutation(np.resize(levels, 8))
        for g in range(8):
            far = levels[np.abs(levels - a[p, g]) >= 10]
            a[p, g + 8] = far[np.random.randint(len(far))]
    return np.exp2(a.ravel()).repeat(32)


def f64(x):
    return np.asarray(x).astype(np.float64)


def striped(idx):
    return np.tile(np.asarray(idx).reshape(-1, 16).T, (8, 1)).astype(np.uint16)


def unstriped(offs):
    return offs[:16].T.reshape(-1).astype(np.int64)


E2M1 = np.array([0.0, 0.5, 1.0, 1.5, 2.0, 3.0, 4.0, 6.0, -0.0, -0.5, -1.0, -1.5, -2.0, -3.0, -4.0, -6.0])


def pack_weight(w, fmt):
    k, n = w.shape
    w = f64(np.asarray(w, np.float32).astype(ml_dtypes.bfloat16)).reshape(k // 32, 32, n)
    amax = np.abs(w).max(1)
    if fmt == "e4m3":
        byte = np.frexp(amax)[1] - 1 + 127 - 7
    else:
        mant, ex = np.frexp(amax / 6.0)
        byte = np.where(mant > 0.5, ex, ex - 1) + 127
    byte = np.clip(np.where(amax > 0, byte, 1), 1, 254)
    scaled = (w * np.exp2(127.0 - byte)[:, None, :]).reshape(k, n).astype(np.float32)
    by_word = np.ascontiguousarray(scaled.reshape(k // 512, 128, 4, n).transpose(0, 1, 3, 2))
    if fmt == "e4m3":
        words = by_word.astype(ml_dtypes.float8_e4m3fn).view(np.uint8)
    else:
        c = by_word.astype(ml_dtypes.float4_e2m1fn).view(np.uint8) & 0xF
        words = (c[..., 0::2] | (c[..., 1::2] << 4)).reshape(k // 512, 128, 2 * n)
    return np.ascontiguousarray(words), np.ascontiguousarray(byte.astype(np.uint8).reshape(k // 512, 16, n))


def unpack_weight(words, scales, fmt):
    g, _, n = scales.shape
    words = np.ascontiguousarray(words).reshape(g, 128, n, -1)
    if fmt == "e4m3":
        vals = words.view(ml_dtypes.float8_e4m3fn).astype(np.float64)
    else:
        nib = np.empty((g, 128, n, 4), np.uint8)
        nib[..., 0::2] = words & 0xF
        nib[..., 1::2] = words >> 4
        vals = E2M1[nib]
    vals = vals * np.repeat(np.exp2(scales.astype(np.float64) - 127.0), 8, axis=1)[..., None]
    return vals.transpose(0, 1, 3, 2).reshape(g * 512, n)


def sigmoid(v):
    return 1.0 / (1.0 + np.exp(-v))


K, T, J, N = 1024, 1024, 512, 512


def setup_inputs():
    n = np.random.standard_normal
    idx = np.random.permutation(T)[:J]
    fk = mx_kscale(K)
    xqp = pack_weight(n((K, T)) / fk[:, None], "e4m3")
    wgp = pack_weight(n((K, N)) * 1 / np.sqrt(K) * fk[:, None], "e2m1")
    return {
        "xq_words": xqp[0],
        "xq_scales": xqp[1],
        "wa": (n((K, N)) * 1 / np.sqrt(K) * fk[:, None]).astype(np.float32),
        "wg_words": wgp[0],
        "wg_scales": wgp[1],
        "res": (1.0 * n((N, T))).astype(np.float32),
        "offs": striped(idx),
    }


def reference(xq_words, xq_scales, wa, wg_words, wg_scales, res, offs):
    idx = unstriped(offs)
    xqu = unpack_weight(xq_words, xq_scales, "e4m3")
    wgu = unpack_weight(wg_words, wg_scales, "e2m1")
    waq = mxq(f64(wa), 0, "e4m3")
    xqidxg = xqu[:, idx]
    p = waq.T @ xqidxg
    g = wgu.T @ xqidxg
    d = p * sigmoid(g)
    dp = np.zeros((N, T))
    dp[:, idx] = d
    y = 0.5 * f64(res) + dp
    return y

@@ -1,0 +1,244 @@
+from contextlib import ExitStack
+
+import concourse.mybir as mybir
+from concourse.masks import make_identity
+
+K, T, J, N = 1024, 1024, 512, 512
+FLOPS = 2 * 2 * K * J * N
+
+F32 = mybir.dt.float32
+BF16 = mybir.dt.bfloat16
+I32 = mybir.dt.int32
+U32 = mybir.dt.uint32
+U16 = mybir.dt.uint16
+U8 = mybir.dt.uint8
+FP8X4 = mybir.dt.float8_e4m3fn_x4
+FP4X4 = mybir.dt.float4_e2m1fn_x4
+MULT = mybir.AluOpType.mult
+ADD = mybir.AluOpType.add
+SIGMOID = mybir.ActivationFunctionType.Sigmoid
+COPY = mybir.ActivationFunctionType.Copy
+
+P = 128
+PACK = 4
+PASSES = K // (P * PACK)
+TILES = N // P
+BANK = 512
+LANES = 16
+HALF = J // 2
+GATE_N = 128
+
+
+def tile_list_expert_self_gate_kernel(tc, xq_words, xq_scales, wa, wg_words, wg_scales, res, offs, out):
+    nc = tc.nc
+    with ExitStack() as ctx:
+        keep = ctx.enter_context(tc.tile_pool(name="keep", bufs=1))
+        psum = ctx.enter_context(tc.psum_pool(name="psum", bufs=1))
+
+        def held(name, shape, dtype, tag=None):
+            return keep.tile(shape, dtype, name=name, tag=tag or name, align_bytes=64)
+
+        def bank(name, number, width):
+            return psum.tile([P, width], F32, name=name, tag="bank%d" % number)
+
+        offsets = held("offsets", [P, J // LANES], U16)
+        x_words = [held("x_words%d" % z, [P, T], I32) for z in range(PASSES)]
+        x_scales = held("x_scales", [P, PASSES * T], U8)
+        g_words = held("g_words", [P, PASSES * 2 * N], U8)
+        g_scales = held("g_scales", [P, PASSES * N], U8)
+        picked_words = [held("picked_words%d" % z, [P, J], U32) for z in range(PASSES)]
+        picked_scales = [held("picked_scales%d" % z, [P, J], U8) for z in range(PASSES)]
+        wa_raw = [[held("wa_raw%d_%d" % (i, z), [P, PACK, P], F32) for z in range(PASSES)] for i in range(TILES)]
+        wa_bf = [held("wa_bf%d" % i, [P, PASSES * P * PACK], BF16) for i in range(TILES)]
+        wa_codes = [held("wa_codes%d" % i, [P, PASSES * P], U32) for i in range(TILES)]
+        wa_scales = [held("wa_scales%d" % i, [P, PASSES * P], U8) for i in range(TILES)]
+        res_sb = [held("res%d" % i, [P, T], F32) for i in range(TILES)]
+        pages = [held("page%d" % i, [P, T], F32) for i in range(TILES - 1)]
+        zero = held("zero", [P, 1], F32)
+        half = held("half", [P, 1], F32)
+        ident = held("ident", [P, P], F32)
+
+        def load_scales(queue, plane, rows):
+            for q in range(4):
+                queue.dma_start(
+                    plane[32 * q : 32 * q + 4, :].bitcast(I32).rearrange("r (z c) -> r z c", z=PASSES),
+                    rows[:, 4 * q : 4 * q + 4, :].bitcast(I32).rearrange("z r c -> r z c"),
+                )
+
+        nc.gpsimd.memset(x_scales[:].bitcast(I32), 0)
+        nc.vector.memset(zero[:], 0.0)
+        nc.gpsimd.memset(g_scales[:].bitcast(I32), 0)
+        load_scales(nc.gpsimd, g_scales, wg_scales)
+        nc.scalar.activation(half[:], zero[:], SIGMOID)
+        nc.gpsimd.memset(pages[0][:], 0.0)
+        make_identity(nc, ident[:])
+        for page in pages[1:]:
+            nc.gpsimd.memset(page[:], 0.0)
+
+        def load_words(z):
+            nc.sync.dma_start(x_words[z][:], xq_words[z].rearrange("p n t -> p (n t)").bitcast(I32))
+
+        def load_wa(i, z):
+            rows = wa[z * P * PACK : (z + 1) * P * PACK, i * P : (i + 1) * P]
+            nc.sync.dma_start(wa_raw[i][z][:], rows.rearrange("(p j) c -> p j c", j=PACK))
+
+        def load_res(i):
+            nc.sync.dma_start(res_sb[i][:], res[i * P : (i + 1) * P, :])
+
+        nc.sync.dma_start(offsets[:], offs)
+        load_words(0)
+        load_scales(nc.sync, x_scales, xq_scales)
+        load_wa(0, 0)
+        load_wa(0, 1)
+        load_words(1)
+        nc.sync.dma_start(
+            g_words[:].bitcast(I32).rearrange("p (z c) -> p z c", z=PASSES),
+            wg_words.bitcast(I32).rearrange("z p c -> p z c"),
+        )
+        for i in range(1, TILES):
+            for z in range(PASSES):
+                load_wa(i, z)
+        for i in range(TILES):
+            load_res(i)
+
+        def entries(j0, j1):
+            return offsets[:, j0 // LANES : j1 // LANES]
+
+        def gather_words(z, j0, j1):
+            nc.vector.tensor_copy(picked_words[z][:, j0:j1], x_words[z][:].bitcast(U32).indirect(entries(j0, j1)))
+
+        def gather_scales(z):
+            nc.vector.tensor_copy(picked_scales[z][:], x_scales[:, z * T : (z + 1) * T].indirect(entries(0, J)))
+
+        def interleave(i):
+            for z in range(PASSES):
+                dst = wa_bf[i][:, z * P * PACK : (z + 1) * P * PACK]
+                nc.scalar.copy(
+                    dst.rearrange("p (c i t) -> p c t i", i=4, t=PACK),
+                    wa_raw[i][z][:].rearrange("p t (c i) -> p c t i", i=4),
+                )
+
+        def quantise(i):
+            nc.vector.quantize_mx(wa_codes[i][:].bitcast(FP8X4), wa_scales[i][:], wa_bf[i][:])
+
+        def gate_product(i, j0, j1, number):
+            width = j1 - j0
+            gate = bank("gate%d_%d" % (i, j0), number, width)
+            step = width if width == BANK else GATE_N
+            for z in range(PASSES):
+                n0 = z * N + i * P
+                for c0 in range(0, width, step):
+                    cols = slice(j0 + c0, j0 + c0 + step)
+                    nc.tensor.matmul_mx(
+                        gate[:, c0 : c0 + step],
+                        lhsT=g_words[:, 2 * n0 : 2 * (n0 + P)].bitcast(FP4X4),
+                        lhsT_scale=g_scales[:, n0 : n0 + P],
+                        rhs=picked_words[z][:, cols].bitcast(FP8X4),
+                        rhs_scale=picked_scales[z][:, cols],
+                        start=(z == 0 and c0 == 0),
+                        stop=(z == PASSES - 1 and c0 + step == width),
+                    )
+            return gate
+
+        def answer_product(i, j0, j1, number):
+            answer = bank("answer%d_%d" % (i, j0), number, j1 - j0)
+            for z in range(PASSES):
+                nc.tensor.matmul_mx(
+                    answer[:],
+                    lhsT=wa_codes[i][:, z * P : (z + 1) * P].bitcast(FP8X4),
+                    lhsT_scale=wa_scales[i][:, z * P : (z + 1) * P],
+                    rhs=picked_words[z][:, j0:j1].bitcast(FP8X4),
+                    rhs_scale=picked_scales[z][:, j0:j1],
+                    start=(z == 0),
+                    stop=(z == PASSES - 1),
+                )
+            return answer
+
+        def leave_psum(gate, answer, gate_sb, answer_sb, factor):
+            nc.scalar.activation(gate_sb, gate, SIGMOID)
+            nc.scalar.activation(answer_sb, answer, COPY, scale=factor)
+            return answer_sb, gate_sb
+
+        def leave_half(name, gate, answer, tag):
+            pair = held(name, [P, 2 * HALF], F32, tag)
+            return leave_psum(gate, answer, pair[:, :HALF], pair[:, HALF:], 2.0)
+
+        def leave_whole(i, gate, answer, gate_tag, answer_tag, factor):
+            gate_sb = held("gate_sb%d" % i, [P, J], F32, gate_tag)
+            answer_sb = held("answer_sb%d" % i, [P, J], F32, answer_tag)
+            return leave_psum(gate[:], answer[:], gate_sb[:], answer_sb[:], factor)
+
+        def scatter(page, j0, j1, pair):
+            nc.vector.tensor_tensor(page[:].indirect(entries(j0, j1)), pair[0], pair[1], MULT)
+
+        def add_on_tensor(i, page, b_turn, b_back, tags):
+            blocks = BANK // P
+            sums = []
+            for b in range(T // BANK):
+                turned = bank("turned%d_%d" % (i, b), b_turn[b], BANK)
+                for src, first in ((res_sb[i], True), (page, False)):
+                    for q in range(blocks):
+                        t0 = b * BANK + q * P
+                        nc.tensor.matmul(
+                            turned[:, q * P : (q + 1) * P],
+                            lhsT=src[:, t0 : t0 + P],
+                            rhs=ident[:],
+                            is_transpose=True,
+                            start=(first and q == 0),
+                            stop=(not first and q == blocks - 1),
+                        )
+                turned_sb = held("turned_sb%d_%d" % (i, b), [P, BANK], F32, tags[b])
+                nc.scalar.copy(turned_sb[:], turned[:])
+                sums.append(turned_sb)
+            for b in range(T // BANK):
+                back = bank("back%d_%d" % (i, b), b_back[b], BANK)
+                for q in range(blocks):
+                    nc.tensor.transpose(back[:, q * P : (q + 1) * P], sums[b][:, q * P : (q + 1) * P], ident[:])
+                result = held("result%d_%d" % (i, b), [P, BANK], F32)
+                nc.scalar.activation(result[:], back[:], COPY, scale=half[:])
+                nc.sync.dma_start(out[i * P : (i + 1) * P, b * BANK : (b + 1) * BANK], result[:])
+
+        def add_on_vector(i, page, tag):
+            result = held("result%d" % i, [P, T], F32, tag)
+            for b in range(T // BANK):
+                cols = slice(b * BANK, (b + 1) * BANK)
+                nc.vector.scalar_tensor_tensor(result[:, cols], res_sb[i][:, cols], half[:], page[:, cols], MULT, ADD)
+                nc.sync.dma_start(out[i * P : (i + 1) * P, cols], result[:, cols])
+
+        interleave(0)
+        gather_words(0, 0, J)
+        gather_scales(0)
+        gather_scales(1)
+        quantise(0)
+        gather_words(1, 0, HALF)
+        gather_words(1, HALF, J)
+        interleave(1)
+        quantise(1)
+        gate = gate_product(0, 0, HALF, 0)
+        answer = answer_product(0, 0, HALF, 1)
+        pair0a = leave_half("pair0a", gate[:], answer[:], "wa_raw1_1")
+        interleave(2)
+        gate = gate_product(0, HALF, J, 2)
+        answer = answer_product(0, HALF, J, 3)
+        pair0b = leave_half("pair0b", gate[:], answer[:], "wa_raw2_1")
+        scatter(pages[0], 0, HALF, pair0a)
+        quantise(2)
+        gate = gate_product(1, 0, J, 3)
+        answer = answer_product(1, 0, J, 4)
+        interleave(3)
+        pair1 = leave_whole(1, gate, answer, "wa_raw3_0", "wa_raw3_1", 2.0)
+        scatter(pages[0], HALF, J, pair0b)
+        quantise(3)
+        gate = gate_product(2, 0, J, 3)
+        answer = answer_product(2, 0, J, 4)
+        pair2 = leave_whole(2, gate, answer, None, None, 2.0)
+        scatter(pages[1], 0, J, pair1)
+        gate = gate_product(3, 0, J, 3)
+        answer = answer_product(3, 0, J, 2)
+        pair3 = leave_whole(3, gate, answer, None, None, 1.0)
+        add_on_tensor(0, pages[0], [0, 1], [6, 7], [None, None])
+        add_on_tensor(1, pages[1], [0, 1], [5, 2], [None, None])
+        scatter(pages[2], 0, J, pair2)
+        add_on_tensor(2, pages[2], [0, 1], [6, 7], ["last", None])
+        scatter(pages[0], 0, J, pair3)
+        add_on_vector(3, pages[0], "last")

@@ -44,7 +44,8 @@ def tile_list_expert_self_gate_kernel(tc, xq_words, xq_scales, wa, wg_words, wg_
         offsets = held("offsets", [P, J // LANES], U16)
         x_words = [held("x_words%d" % z, [P, T], I32) for z in range(PASSES)]
         x_scales = held("x_scales", [P, PASSES * T], U8)
-        g_words = held("g_words", [P, PASSES * 2 * N], U8)
+        g_first = held("g_first", [P, PASSES * 2 * P], U8)
+        g_rest = held("g_rest", [P, PASSES * 2 * (N - P)], U8)
         g_scales = held("g_scales", [P, PASSES * N], U8)
         picked_words = [held("picked_words%d" % z, [P, J], U32) for z in range(PASSES)]
         picked_scales = [held("picked_scales%d" % z, [P, J], U8) for z in range(PASSES)]
@@ -67,8 +68,7 @@ def tile_list_expert_self_gate_kernel(tc, xq_words, xq_scales, wa, wg_words, wg_
 
         nc.gpsimd.memset(x_scales[:].bitcast(I32), 0)
         nc.vector.memset(zero[:], 0.0)
-        nc.gpsimd.memset(g_scales[:].bitcast(I32), 0)
-        load_scales(nc.gpsimd, g_scales, wg_scales)
+        nc.vector.memset(g_scales[:].bitcast(I32), 0)
         nc.scalar.activation(half[:], zero[:], SIGMOID)
         nc.gpsimd.memset(pages[0][:], 0.0)
         make_identity(nc, ident[:])
@@ -82,6 +82,18 @@ def tile_list_expert_self_gate_kernel(tc, xq_words, xq_scales, wa, wg_words, wg_
             rows = wa[z * P * PACK : (z + 1) * P * PACK, i * P : (i + 1) * P]
             nc.sync.dma_start(wa_raw[i][z][:], rows.rearrange("(p j) c -> p j c", j=PACK))
 
+        def load_gate_words(tile, n0, n1):
+            nc.sync.dma_start(
+                tile[:].bitcast(I32).rearrange("p (z c) -> p z c", z=PASSES),
+                wg_words[:, :, 2 * n0 : 2 * n1].bitcast(I32).rearrange("z p c -> p z c"),
+            )
+
+        def gate_weights(i, z):
+            if i == 0:
+                return g_first[:, 2 * z * P : 2 * (z + 1) * P]
+            c0 = z * (N - P) + (i - 1) * P
+            return g_rest[:, 2 * c0 : 2 * (c0 + P)]
+
         def load_res(i):
             nc.sync.dma_start(res_sb[i][:], res[i * P : (i + 1) * P, :])
 
@@ -90,12 +102,13 @@ def tile_list_expert_self_gate_kernel(tc, xq_words, xq_scales, wa, wg_words, wg_
         load_scales(nc.sync, x_scales, xq_scales)
         load_wa(0, 0)
         load_wa(0, 1)
+        load_gate_words(g_first, 0, P)
+        load_scales(nc.sync, g_scales, wg_scales)
         load_words(1)
-        nc.sync.dma_start(
-            g_words[:].bitcast(I32).rearrange("p (z c) -> p z c", z=PASSES),
-            wg_words.bitcast(I32).rearrange("z p c -> p z c"),
-        )
-        for i in range(1, TILES):
+        load_wa(1, 0)
+        load_wa(1, 1)
+        load_gate_words(g_rest, P, N)
+        for i in range(2, TILES):
             for z in range(PASSES):
                 load_wa(i, z)
         for i in range(TILES):
@@ -131,7 +144,7 @@ def tile_list_expert_self_gate_kernel(tc, xq_words, xq_scales, wa, wg_words, wg_
                     cols = slice(j0 + c0, j0 + c0 + step)
                     nc.tensor.matmul_mx(
                         gate[:, c0 : c0 + step],
-                        lhsT=g_words[:, 2 * n0 : 2 * (n0 + P)].bitcast(FP4X4),
+                        lhsT=gate_weights(i, z).bitcast(FP4X4),
                         lhsT_scale=g_scales[:, n0 : n0 + P],
                         rhs=picked_words[z][:, cols].bitcast(FP8X4),
                         rhs_scale=picked_scales[z][:, cols],
@@ -200,16 +213,16 @@ def tile_list_expert_self_gate_kernel(tc, xq_words, xq_scales, wa, wg_words, wg_
 
         def add_on_vector(i, page, tag):
             result = held("result%d" % i, [P, T], F32, tag)
-            for b in range(T // BANK):
-                cols = slice(b * BANK, (b + 1) * BANK)
+            for t0, t1 in ((0, T // 2), (T // 2, 3 * T // 4), (3 * T // 4, T)):
+                cols = slice(t0, t1)
                 nc.vector.scalar_tensor_tensor(result[:, cols], res_sb[i][:, cols], half[:], page[:, cols], MULT, ADD)
                 nc.sync.dma_start(out[i * P : (i + 1) * P, cols], result[:, cols])
 
         interleave(0)
         gather_words(0, 0, J)
         gather_scales(0)
-        gather_scales(1)
         quantise(0)
+        gather_scales(1)
         gather_words(1, 0, HALF)
         gather_words(1, HALF, J)
         interleave(1)
@@ -218,27 +231,28 @@ def tile_list_expert_self_gate_kernel(tc, xq_words, xq_scales, wa, wg_words, wg_
         answer = answer_product(0, 0, HALF, 1)
         pair0a = leave_half("pair0a", gate[:], answer[:], "wa_raw1_1")
         interleave(2)
-        gate = gate_product(0, HALF, J, 2)
-        answer = answer_product(0, HALF, J, 3)
+        gate = gate_product(0, HALF, J, 0)
+        answer = answer_product(0, HALF, J, 1)
         pair0b = leave_half("pair0b", gate[:], answer[:], "wa_raw2_1")
         scatter(pages[0], 0, HALF, pair0a)
         quantise(2)
-        gate = gate_product(1, 0, J, 3)
-        answer = answer_product(1, 0, J, 4)
+        gate = gate_product(1, 0, J, 2)
+        answer = answer_product(1, 0, J, 3)
         interleave(3)
         pair1 = leave_whole(1, gate, answer, "wa_raw3_0", "wa_raw3_1", 2.0)
         scatter(pages[0], HALF, J, pair0b)
         quantise(3)
-        gate = gate_product(2, 0, J, 3)
+        late = held("late", [P, 3 * J], F32, "wa_bf3")
+        gate = gate_product(2, 0, J, 0)
         answer = answer_product(2, 0, J, 4)
-        pair2 = leave_whole(2, gate, answer, None, None, 2.0)
+        pair2 = leave_psum(gate[:], answer[:], late[:, :J], late[:, J : 2 * J], 2.0)
         scatter(pages[1], 0, J, pair1)
-        gate = gate_product(3, 0, J, 3)
-        answer = answer_product(3, 0, J, 2)
-        pair3 = leave_whole(3, gate, answer, None, None, 1.0)
-        add_on_tensor(0, pages[0], [0, 1], [6, 7], [None, None])
-        add_on_tensor(1, pages[1], [0, 1], [5, 2], [None, None])
+        gate = gate_product(3, 0, J, 1)
+        answer = answer_product(3, 0, J, 5)
+        pair3 = leave_psum(gate[:], answer[:], late[:, 2 * J :], held("answer_sb3", [P, J], F32)[:], 1.0)
+        add_on_tensor(0, pages[0], [6, 7], [2, 3], [None, None])
+        add_on_tensor(1, pages[1], [6, 7], [4, 5], [None, None])
         scatter(pages[2], 0, J, pair2)
-        add_on_tensor(2, pages[2], [0, 1], [6, 7], ["last", None])
+        add_on_tensor(2, pages[2], [6, 7], [0, 1], ["last", None])
         scatter(pages[0], 0, J, pair3)
         add_on_vector(3, pages[0], "last")

from contextlib import ExitStack

import concourse.mybir as mybir
from concourse.masks import make_identity

K, T, J, N = 1024, 1024, 512, 512
FLOPS = 2 * 2 * K * J * N

F32 = mybir.dt.float32
BF16 = mybir.dt.bfloat16
I32 = mybir.dt.int32
U32 = mybir.dt.uint32
U16 = mybir.dt.uint16
U8 = mybir.dt.uint8
FP8X4 = mybir.dt.float8_e4m3fn_x4
FP4X4 = mybir.dt.float4_e2m1fn_x4
MULT = mybir.AluOpType.mult
ADD = mybir.AluOpType.add
SIGMOID = mybir.ActivationFunctionType.Sigmoid
COPY = mybir.ActivationFunctionType.Copy

P = 128
PACK = 4
PASSES = K // (P * PACK)
TILES = N // P
BANK = 512
LANES = 16
HALF = J // 2
GATE_N = 128


def tile_list_expert_self_gate_kernel(tc, xq_words, xq_scales, wa, wg_words, wg_scales, res, offs, out):
    nc = tc.nc
    with ExitStack() as ctx:
        keep = ctx.enter_context(tc.tile_pool(name="keep", bufs=1))
        psum = ctx.enter_context(tc.psum_pool(name="psum", bufs=1))

        def held(name, shape, dtype, tag=None):
            return keep.tile(shape, dtype, name=name, tag=tag or name, align_bytes=64)

        def bank(name, number, width):
            return psum.tile([P, width], F32, name=name, tag="bank%d" % number)

        offsets = held("offsets", [P, J // LANES], U16)
        x_words = [held("x_words%d" % z, [P, T], I32) for z in range(PASSES)]
        x_scales = held("x_scales", [P, PASSES * T], U8)
        g_first = held("g_first", [P, PASSES * 2 * P], U8)
        g_rest = held("g_rest", [P, PASSES * 2 * (N - P)], U8)
        g_scales = held("g_scales", [P, PASSES * N], U8)
        picked_words = [held("picked_words%d" % z, [P, J], U32) for z in range(PASSES)]
        picked_scales = [held("picked_scales%d" % z, [P, J], U8) for z in range(PASSES)]
        wa_raw = [[held("wa_raw%d_%d" % (i, z), [P, PACK, P], F32) for z in range(PASSES)] for i in range(TILES)]
        wa_bf = [held("wa_bf%d" % i, [P, PASSES * P * PACK], BF16) for i in range(TILES)]
        wa_codes = [held("wa_codes%d" % i, [P, PASSES * P], U32) for i in range(TILES)]
        wa_scales = [held("wa_scales%d" % i, [P, PASSES * P], U8) for i in range(TILES)]
        res_sb = [held("res%d" % i, [P, T], F32) for i in range(TILES)]
        pages = [held("page%d" % i, [P, T], F32) for i in range(TILES - 1)]
        zero = held("zero", [P, 1], F32)
        half = held("half", [P, 1], F32)
        ident = held("ident", [P, P], F32)

        def load_scales(queue, plane, rows):
            for q in range(4):
                queue.dma_start(
                    plane[32 * q : 32 * q + 4, :].bitcast(I32).rearrange("r (z c) -> r z c", z=PASSES),
                    rows[:, 4 * q : 4 * q + 4, :].bitcast(I32).rearrange("z r c -> r z c"),
                )

        nc.gpsimd.memset(x_scales[:].bitcast(I32), 0)
        nc.vector.memset(zero[:], 0.0)
        nc.vector.memset(g_scales[:].bitcast(I32), 0)
        nc.scalar.activation(half[:], zero[:], SIGMOID)
        nc.gpsimd.memset(pages[0][:], 0.0)
        make_identity(nc, ident[:])
        for page in pages[1:]:
            nc.gpsimd.memset(page[:], 0.0)

        def load_words(z):
            nc.sync.dma_start(x_words[z][:], xq_words[z].rearrange("p n t -> p (n t)").bitcast(I32))

        def load_wa(i, z):
            rows = wa[z * P * PACK : (z + 1) * P * PACK, i * P : (i + 1) * P]
            nc.sync.dma_start(wa_raw[i][z][:], rows.rearrange("(p j) c -> p j c", j=PACK))

        def load_gate_words(tile, n0, n1):
            nc.sync.dma_start(
                tile[:].bitcast(I32).rearrange("p (z c) -> p z c", z=PASSES),
                wg_words[:, :, 2 * n0 : 2 * n1].bitcast(I32).rearrange("z p c -> p z c"),
            )

        def gate_weights(i, z):
            if i == 0:
                return g_first[:, 2 * z * P : 2 * (z + 1) * P]
            c0 = z * (N - P) + (i - 1) * P
            return g_rest[:, 2 * c0 : 2 * (c0 + P)]

        def load_res(i):
            nc.sync.dma_start(res_sb[i][:], res[i * P : (i + 1) * P, :])

        nc.sync.dma_start(offsets[:], offs)
        load_words(0)
        load_scales(nc.sync, x_scales, xq_scales)
        load_wa(0, 0)
        load_wa(0, 1)
        load_gate_words(g_first, 0, P)
        load_scales(nc.sync, g_scales, wg_scales)
        load_words(1)
        load_wa(1, 0)
        load_wa(1, 1)
        load_gate_words(g_rest, P, N)
        for i in range(2, TILES):
            for z in range(PASSES):
                load_wa(i, z)
        for i in range(TILES):
            load_res(i)

        def entries(j0, j1):
            return offsets[:, j0 // LANES : j1 // LANES]

        def gather_words(z, j0, j1):
            nc.vector.tensor_copy(picked_words[z][:, j0:j1], x_words[z][:].bitcast(U32).indirect(entries(j0, j1)))

        def gather_scales(z):
            nc.vector.tensor_copy(picked_scales[z][:], x_scales[:, z * T : (z + 1) * T].indirect(entries(0, J)))

        def interleave(i):
            for z in range(PASSES):
                dst = wa_bf[i][:, z * P * PACK : (z + 1) * P * PACK]
                nc.scalar.copy(
                    dst.rearrange("p (c i t) -> p c t i", i=4, t=PACK),
                    wa_raw[i][z][:].rearrange("p t (c i) -> p c t i", i=4),
                )

        def quantise(i):
            nc.vector.quantize_mx(wa_codes[i][:].bitcast(FP8X4), wa_scales[i][:], wa_bf[i][:])

        def gate_product(i, j0, j1, number):
            width = j1 - j0
            gate = bank("gate%d_%d" % (i, j0), number, width)
            step = width if width == BANK else GATE_N
            for z in range(PASSES):
                n0 = z * N + i * P
                for c0 in range(0, width, step):
                    cols = slice(j0 + c0, j0 + c0 + step)
                    nc.tensor.matmul_mx(
                        gate[:, c0 : c0 + step],
                        lhsT=gate_weights(i, z).bitcast(FP4X4),
                        lhsT_scale=g_scales[:, n0 : n0 + P],
                        rhs=picked_words[z][:, cols].bitcast(FP8X4),
                        rhs_scale=picked_scales[z][:, cols],
                        start=(z == 0 and c0 == 0),
                        stop=(z == PASSES - 1 and c0 + step == width),
                    )
            return gate

        def answer_product(i, j0, j1, number):
            answer = bank("answer%d_%d" % (i, j0), number, j1 - j0)
            for z in range(PASSES):
                nc.tensor.matmul_mx(
                    answer[:],
                    lhsT=wa_codes[i][:, z * P : (z + 1) * P].bitcast(FP8X4),
                    lhsT_scale=wa_scales[i][:, z * P : (z + 1) * P],
                    rhs=picked_words[z][:, j0:j1].bitcast(FP8X4),
                    rhs_scale=picked_scales[z][:, j0:j1],
                    start=(z == 0),
                    stop=(z == PASSES - 1),
                )
            return answer

        def leave_psum(gate, answer, gate_sb, answer_sb, factor):
            nc.scalar.activation(gate_sb, gate, SIGMOID)
            nc.scalar.activation(answer_sb, answer, COPY, scale=factor)
            return answer_sb, gate_sb

        def leave_half(name, gate, answer, tag):
            pair = held(name, [P, 2 * HALF], F32, tag)
            return leave_psum(gate, answer, pair[:, :HALF], pair[:, HALF:], 2.0)

        def leave_whole(i, gate, answer, gate_tag, answer_tag, factor):
            gate_sb = held("gate_sb%d" % i, [P, J], F32, gate_tag)
            answer_sb = held("answer_sb%d" % i, [P, J], F32, answer_tag)
            return leave_psum(gate[:], answer[:], gate_sb[:], answer_sb[:], factor)

        def scatter(page, j0, j1, pair):
            nc.vector.tensor_tensor(page[:].indirect(entries(j0, j1)), pair[0], pair[1], MULT)

        def add_on_tensor(i, page, b_turn, b_back, tags):
            blocks = BANK // P
            sums = []
            for b in range(T // BANK):
                turned = bank("turned%d_%d" % (i, b), b_turn[b], BANK)
                for src, first in ((res_sb[i], True), (page, False)):
                    for q in range(blocks):
                        t0 = b * BANK + q * P
                        nc.tensor.matmul(
                            turned[:, q * P : (q + 1) * P],
                            lhsT=src[:, t0 : t0 + P],
                            rhs=ident[:],
                            is_transpose=True,
                            start=(first and q == 0),
                            stop=(not first and q == blocks - 1),
                        )
                turned_sb = held("turned_sb%d_%d" % (i, b), [P, BANK], F32, tags[b])
                nc.scalar.copy(turned_sb[:], turned[:])
                sums.append(turned_sb)
            for b in range(T // BANK):
                back = bank("back%d_%d" % (i, b), b_back[b], BANK)
                for q in range(blocks):
                    nc.tensor.transpose(back[:, q * P : (q + 1) * P], sums[b][:, q * P : (q + 1) * P], ident[:])
                result = held("result%d_%d" % (i, b), [P, BANK], F32)
                nc.scalar.activation(result[:], back[:], COPY, scale=half[:])
                nc.sync.dma_start(out[i * P : (i + 1) * P, b * BANK : (b + 1) * BANK], result[:])

        def add_on_vector(i, page, tag):
            result = held("result%d" % i, [P, T], F32, tag)
            for t0, t1 in ((0, T // 2), (T // 2, 3 * T // 4), (3 * T // 4, T)):
                cols = slice(t0, t1)
                nc.vector.scalar_tensor_tensor(result[:, cols], res_sb[i][:, cols], half[:], page[:, cols], MULT, ADD)
                nc.sync.dma_start(out[i * P : (i + 1) * P, cols], result[:, cols])

        interleave(0)
        gather_words(0, 0, J)
        gather_scales(0)
        quantise(0)
        gather_scales(1)
        gather_words(1, 0, HALF)
        gather_words(1, HALF, J)
        interleave(1)
        quantise(1)
        gate = gate_product(0, 0, HALF, 0)
        answer = answer_product(0, 0, HALF, 1)
        pair0a = leave_half("pair0a", gate[:], answer[:], "wa_raw1_1")
        interleave(2)
        gate = gate_product(0, HALF, J, 0)
        answer = answer_product(0, HALF, J, 1)
        pair0b = leave_half("pair0b", gate[:], answer[:], "wa_raw2_1")
        scatter(pages[0], 0, HALF, pair0a)
        quantise(2)
        gate = gate_product(1, 0, J, 2)
        answer = answer_product(1, 0, J, 3)
        interleave(3)
        pair1 = leave_whole(1, gate, answer, "wa_raw3_0", "wa_raw3_1", 2.0)
        scatter(pages[0], HALF, J, pair0b)
        quantise(3)
        late = held("late", [P, 3 * J], F32, "wa_bf3")
        gate = gate_product(2, 0, J, 0)
        answer = answer_product(2, 0, J, 4)
        pair2 = leave_psum(gate[:], answer[:], late[:, :J], late[:, J : 2 * J], 2.0)
        scatter(pages[1], 0, J, pair1)
        gate = gate_product(3, 0, J, 1)
        answer = answer_product(3, 0, J, 5)
        pair3 = leave_psum(gate[:], answer[:], late[:, 2 * J :], held("answer_sb3", [P, J], F32)[:], 1.0)
        add_on_tensor(0, pages[0], [6, 7], [2, 3], [None, None])
        add_on_tensor(1, pages[1], [6, 7], [4, 5], [None, None])
        scatter(pages[2], 0, J, pair2)
        add_on_tensor(2, pages[2], [6, 7], [0, 1], ["last", None])
        scatter(pages[0], 0, J, pair3)
        add_on_vector(3, pages[0], "last")
